import numpy as np
import ml_dtypes


def mxq(x, axis, fmt="e4m3"):
    dtype, down = {"e4m3": (ml_dtypes.float8_e4m3fn, 7), "e5m2": (ml_dtypes.float8_e5m2, 14)}[fmt]
    v = np.moveaxis(np.asarray(x, np.float32).astype(ml_dtypes.bfloat16).astype(np.float64), axis, -1)
    blocks = v.reshape(v.shape[:-1] + (-1, 32))
    amax = np.abs(blocks).max(-1, keepdims=True)
    byte = np.maximum(np.where(amax > 0, np.frexp(amax)[1] - 1 + 127, 0) - down, 1)
    scale = np.exp2(byte - 127.0)
    codes = (blocks / scale).astype(np.float32).astype(dtype).astype(np.float64)
    return np.moveaxis((codes * scale).reshape(v.shape), -1, axis)


WIDE = False


def mx_kscale(k):
    if not WIDE:
        return np.ones(k)
    levels = np.array([10, -10, 5, -5, 0])
    if k % 512:
        return np.exp2(np.random.permutation(np.resize(levels, k // 32))).repeat(32)
    a = np.empty((k // 512, 16))
    for p in range(k // 512):
        a[p, :8] = np.random.permutation(np.resize(levels, 8))
        for g in range(8):
            far = levels[np.abs(levels - a[p, g]) >= 10]
            a[p, g + 8] = far[np.random.randint(len(far))]
    return np.exp2(a.ravel()).repeat(32)


def f64(x):
    return np.asarray(x).astype(np.float64)


def striped(idx):
    return np.tile(idx.reshape(-1, 16).T, (8, 1)).astype(np.uint16)


def unstriped(offs):
    return offs[:16].T.reshape(-1).astype(np.int64)


def pack_weight(w):
    k, n = w.shape
    w = f64(np.asarray(w, np.float32).astype(ml_dtypes.bfloat16)).reshape(k // 32, 32, n)
    amax = np.abs(w).max(1)
    byte = np.clip(np.where(amax > 0, np.frexp(amax)[1] - 1 + 127 - 7, 1), 1, 254)
    scaled = (w * np.exp2(127.0 - byte)[:, None, :]).reshape(k, n).astype(np.float32)
    words = np.ascontiguousarray(scaled.reshape(k // 512, 128, 4, n).transpose(0, 1, 3, 2)).astype(ml_dtypes.float8_e4m3fn).view(np.uint8)
    return words, np.ascontiguousarray(byte.astype(np.uint8).reshape(k // 512, 16, n))


def unpack_weight(words, scales):
    g, p, n, _ = words.shape
    vals = np.ascontiguousarray(words).view(ml_dtypes.float8_e4m3fn).astype(np.float64) * np.repeat(np.exp2(scales.astype(np.float64) - 127.0), 8, axis=1)[..., None]
    return vals.transpose(0, 1, 3, 2).reshape(g * 512, n)


K, T, S, N = 512, 256, 512, 1024


def setup_inputs():
    n = np.random.standard_normal
    s = mx_kscale(K)[:, None]
    packed = pack_weight(n((K, N)) / np.sqrt(K) / s)
    return {
        "w_words": packed[0],
        "w_scales": packed[1],
        "xT": (n((K, T)) * s).astype(np.float32),
        "b": (0.3 * n((S, 1))).astype(np.float32),
        "offs": striped(np.sort(np.random.permutation(N)[:S])),
    }


def reference(w_words, w_scales, xT, b, offs):
    idx = unstriped(offs)
    wq = unpack_weight(w_words, w_scales)[:, idx]
    return (wq.T @ mxq(f64(xT), 0, "e4m3")) + f64(b)

@@ -1,0 +1,96 @@
+from contextlib import ExitStack
+
+import concourse.mybir as mybir
+
+K, T, S, N = 512, 256, 512, 1024
+FLOPS = 2 * K * S * T
+
+F32 = mybir.dt.float32
+BF16 = mybir.dt.bfloat16
+I32 = mybir.dt.int32
+U32 = mybir.dt.uint32
+U16 = mybir.dt.uint16
+U8 = mybir.dt.uint8
+FP8X4 = mybir.dt.float8_e4m3fn_x4
+IDENT = mybir.ActivationFunctionType.Identity
+ADD = mybir.AluOpType.add
+
+P = 128
+PACK = 4
+M = 128
+CHUNKS = S // M
+COLS = M // 16
+W_FIRST = 768
+HALF = T // 2
+
+
+def tile_picked_neuron_lin_bias_srt_p_kernel(tc, w_words, w_scales, xT, b, offs, out):
+    nc = tc.nc
+    with ExitStack() as ctx:
+        keep = ctx.enter_context(tc.tile_pool(name="keep", bufs=1))
+        psum = ctx.enter_context(tc.psum_pool(name="psum", bufs=1))
+
+        offsets = keep.tile([P, S // 16], U16, name="offsets")
+        nc.sync.dma_start(offsets[:], offs)
+
+        scale_table = keep.tile([P, N], U8, name="scale_table", tag="scale_table_then_x_low", align_bytes=64)
+        nc.vector.memset(scale_table[:].bitcast(I32), 0)
+        for q in range(4):
+            nc.sync.dma_start(scale_table[32 * q : 32 * q + 4, :].bitcast(I32), w_scales[0, 4 * q : 4 * q + 4, :].bitcast(I32))
+
+        x_raw = keep.tile([P, PACK, T], F32, name="x_raw", align_bytes=64)
+        nc.scalar.dma_start(x_raw[:], xT.rearrange("(p j) t -> p j t", j=PACK))
+
+        word_table = keep.tile([P, N], I32, name="word_table", align_bytes=64)
+        w_rows = w_words[0].rearrange("p n r -> p (n r)")
+        for c0, c1 in ((0, W_FIRST), (W_FIRST, N)):
+            nc.scalar.dma_start(word_table[:, c0:c1], w_rows[:, 4 * c0 : 4 * c1].bitcast(I32))
+
+        warm_in = keep.tile([P, 1], F32, name="warm_in", tag="warm_then_bias")
+        warm_out = keep.tile([P, 1], F32, name="warm_out")
+        nc.vector.memset(warm_in[:], 0.0)
+        nc.scalar.activation(warm_out[:], warm_in[:], IDENT)
+
+        bias = keep.tile([P, CHUNKS], F32, name="bias", tag="warm_then_bias")
+        with nc.allow_non_contiguous_dma(reason="one bias value a partition and chunk"):
+            nc.sync.dma_start(bias[:], b.rearrange("(c p) o -> p (c o)", p=P))
+
+        w_scale = keep.tile([P, S], U8, name="w_scale", align_bytes=64)
+        nc.vector.tensor_copy(w_scale[:], scale_table[:].indirect(offsets[:]))
+
+        x_low = keep.tile([P, HALF, PACK], BF16, name="x_low", tag="scale_table_then_x_low", align_bytes=64)
+        x_high = keep.tile([P, HALF, PACK], BF16, name="x_high", align_bytes=64)
+        dst = lambda t: t[:].rearrange("p (c i) j -> p c j i", i=4)
+        src = lambda t0: x_raw[:, :, t0 : t0 + HALF].rearrange("p j (c i) -> p c j i", i=4)
+        nc.vector.tensor_copy(dst(x_low), src(0))
+        nc.scalar.copy(dst(x_high), src(HALF))
+
+        x_codes = keep.tile([P, T], U32, name="x_codes", align_bytes=64)
+        x_scale = keep.tile([P, T], U8, name="x_scale", align_bytes=64)
+        for t0, x_half in ((0, x_low), (HALF, x_high)):
+            nc.vector.quantize_mx(
+                out=x_codes[:, t0 : t0 + HALF].bitcast(FP8X4),
+                scales=x_scale[:, t0 : t0 + HALF],
+                in_=x_half[:].rearrange("p t j -> p (t j)"),
+            )
+
+        w_codes = keep.tile([P, S], U32, name="w_codes", tag="scale_table_then_x_low", align_bytes=64)
+        for m in range(CHUNKS):
+            reach = W_FIRST if M * (m + 1) + (N - S) <= W_FIRST else N
+            nc.vector.tensor_copy(w_codes[:, M * m : M * (m + 1)], word_table[:, 0:reach].bitcast(U32).indirect(offsets[:, COLS * m : COLS * (m + 1)]))
+            acc = psum.tile([M, T], F32, name="acc%d" % m)
+            nc.tensor.matmul_mx(
+                out=acc[:],
+                lhsT=w_codes[:, M * m : M * (m + 1)].bitcast(FP8X4),
+                lhsT_scale=w_scale[:, M * m : M * (m + 1)],
+                rhs=x_codes[:].bitcast(FP8X4),
+                rhs_scale=x_scale[:],
+                start=True,
+                stop=True,
+            )
+            result = keep.tile([M, T], F32, name="result%d" % m)
+            if m < CHUNKS - 1:
+                nc.scalar.activation(result[:], acc[:], IDENT, bias=bias[:, m : m + 1])
+            else:
+                nc.vector.tensor_scalar(result[:], acc[:], bias[:, m : m + 1], None, ADD)
+            nc.sync.dma_start(out[M * m : M * (m + 1), :], result[:])

@@ -20,8 +20,7 @@ PACK = 4
 M = 128
 CHUNKS = S // M
 COLS = M // 16
-W_FIRST = 768
-HALF = T // 2
+W_FIRST = 640
 
 
 def tile_picked_neuron_lin_bias_srt_p_kernel(tc, w_words, w_scales, xT, b, offs, out):
@@ -33,56 +32,49 @@ def tile_picked_neuron_lin_bias_srt_p_kernel(tc, w_words, w_scales, xT, b, offs,
         offsets = keep.tile([P, S // 16], U16, name="offsets")
         nc.sync.dma_start(offsets[:], offs)
 
-        scale_table = keep.tile([P, N], U8, name="scale_table", tag="scale_table_then_x_low", align_bytes=64)
-        nc.vector.memset(scale_table[:].bitcast(I32), 0)
-        for q in range(4):
-            nc.sync.dma_start(scale_table[32 * q : 32 * q + 4, :].bitcast(I32), w_scales[0, 4 * q : 4 * q + 4, :].bitcast(I32))
-
         x_raw = keep.tile([P, PACK, T], F32, name="x_raw", align_bytes=64)
         nc.scalar.dma_start(x_raw[:], xT.rearrange("(p j) t -> p j t", j=PACK))
 
-        word_table = keep.tile([P, N], I32, name="word_table", align_bytes=64)
-        w_rows = w_words[0].rearrange("p n r -> p (n r)")
-        for c0, c1 in ((0, W_FIRST), (W_FIRST, N)):
-            nc.scalar.dma_start(word_table[:, c0:c1], w_rows[:, 4 * c0 : 4 * c1].bitcast(I32))
+        scale_table = keep.tile([P, N], U8, name="scale_table", tag="scale_table_then_x_codes", align_bytes=64)
+        nc.vector.memset(scale_table[:].bitcast(I32), 0)
+        for q in range(4):
+            queue = nc.sync if q % 2 == 0 else nc.scalar
+            queue.dma_start(scale_table[32 * q : 32 * q + 4, :].bitcast(I32), w_scales[0, 4 * q : 4 * q + 4, :].bitcast(I32))
 
-        warm_in = keep.tile([P, 1], F32, name="warm_in", tag="warm_then_bias")
-        warm_out = keep.tile([P, 1], F32, name="warm_out")
+        warm_in = keep.tile([P, 1], F32, name="warm_in", tag="warm_in_then_word_table", align_bytes=64)
+        warm_out = keep.tile([P, 1], F32, name="warm_out", tag="warm_out_then_bias")
         nc.vector.memset(warm_in[:], 0.0)
         nc.scalar.activation(warm_out[:], warm_in[:], IDENT)
 
-        bias = keep.tile([P, CHUNKS], F32, name="bias", tag="warm_then_bias")
+        word_table = keep.tile([P, N], I32, name="word_table", tag="warm_in_then_word_table", align_bytes=64)
+        w_rows = w_words[0].rearrange("p n r -> p (n r)")
+        for c0, c1 in ((0, W_FIRST), (W_FIRST, N)):
+            nc.sync.dma_start(word_table[:, c0:c1], w_rows[:, 4 * c0 : 4 * c1].bitcast(I32))
+
+        bias = keep.tile([P, CHUNKS], F32, name="bias", tag="warm_out_then_bias")
         with nc.allow_non_contiguous_dma(reason="one bias value a partition and chunk"):
             nc.sync.dma_start(bias[:], b.rearrange("(c p) o -> p (c o)", p=P))
 
         w_scale = keep.tile([P, S], U8, name="w_scale", align_bytes=64)
         nc.vector.tensor_copy(w_scale[:], scale_table[:].indirect(offsets[:]))
 
-        x_low = keep.tile([P, HALF, PACK], BF16, name="x_low", tag="scale_table_then_x_low", align_bytes=64)
-        x_high = keep.tile([P, HALF, PACK], BF16, name="x_high", align_bytes=64)
-        dst = lambda t: t[:].rearrange("p (c i) j -> p c j i", i=4)
-        src = lambda t0: x_raw[:, :, t0 : t0 + HALF].rearrange("p j (c i) -> p c j i", i=4)
-        nc.vector.tensor_copy(dst(x_low), src(0))
-        nc.scalar.copy(dst(x_high), src(HALF))
+        x_bf = keep.tile([P, T, PACK], BF16, name="x_bf", tag="x_bf_then_w_codes", align_bytes=64)
+        nc.scalar.copy(x_bf[:].rearrange("p (c i) j -> p c j i", i=4), x_raw[:].rearrange("p j (c i) -> p c j i", i=4))
 
-        x_codes = keep.tile([P, T], U32, name="x_codes", align_bytes=64)
+        x_codes = keep.tile([P, T], U32, name="x_codes", tag="scale_table_then_x_codes", align_bytes=64)
         x_scale = keep.tile([P, T], U8, name="x_scale", align_bytes=64)
-        for t0, x_half in ((0, x_low), (HALF, x_high)):
-            nc.vector.quantize_mx(
-                out=x_codes[:, t0 : t0 + HALF].bitcast(FP8X4),
-                scales=x_scale[:, t0 : t0 + HALF],
-                in_=x_half[:].rearrange("p t j -> p (t j)"),
-            )
+        nc.vector.quantize_mx(out=x_codes[:].bitcast(FP8X4), scales=x_scale[:], in_=x_bf[:].rearrange("p t j -> p (t j)"))
 
-        w_codes = keep.tile([P, S], U32, name="w_codes", tag="scale_table_then_x_low", align_bytes=64)
+        w_codes = keep.tile([P, S], U32, name="w_codes", tag="x_bf_then_w_codes", align_bytes=64)
         for m in range(CHUNKS):
             reach = W_FIRST if M * (m + 1) + (N - S) <= W_FIRST else N
-            nc.vector.tensor_copy(w_codes[:, M * m : M * (m + 1)], word_table[:, 0:reach].bitcast(U32).indirect(offsets[:, COLS * m : COLS * (m + 1)]))
+            cols = slice(M * m, M * (m + 1))
+            nc.vector.tensor_copy(w_codes[:, cols], word_table[:, 0:reach].bitcast(U32).indirect(offsets[:, COLS * m : COLS * (m + 1)]))
             acc = psum.tile([M, T], F32, name="acc%d" % m)
             nc.tensor.matmul_mx(
                 out=acc[:],
-                lhsT=w_codes[:, M * m : M * (m + 1)].bitcast(FP8X4),
-                lhsT_scale=w_scale[:, M * m : M * (m + 1)],
+                lhsT=w_codes[:, cols].bitcast(FP8X4),
+                lhsT_scale=w_scale[:, cols],
                 rhs=x_codes[:].bitcast(FP8X4),
                 rhs_scale=x_scale[:],
                 start=True,
@@ -93,4 +85,4 @@ def tile_picked_neuron_lin_bias_srt_p_kernel(tc, w_words, w_scales, xT, b, offs,
                 nc.scalar.activation(result[:], acc[:], IDENT, bias=bias[:, m : m + 1])
             else:
                 nc.vector.tensor_scalar(result[:], acc[:], bias[:, m : m + 1], None, ADD)
-            nc.sync.dma_start(out[M * m : M * (m + 1), :], result[:])
+            nc.sync.dma_start(out[cols, :], result[:])

@@ -27,6 +27,7 @@ def tile_picked_neuron_lin_bias_srt_p_kernel(tc, w_words, w_scales, xT, b, offs,
     nc = tc.nc
     with ExitStack() as ctx:
         keep = ctx.enter_context(tc.tile_pool(name="keep", bufs=1))
+        shared = ctx.enter_context(tc.tile_pool(name="shared", bufs=1))
         psum = ctx.enter_context(tc.psum_pool(name="psum", bufs=1))
 
         offsets = keep.tile([P, S // 16], U16, name="offsets")
@@ -35,10 +36,10 @@ def tile_picked_neuron_lin_bias_srt_p_kernel(tc, w_words, w_scales, xT, b, offs,
         x_raw = keep.tile([P, PACK, T], F32, name="x_raw", align_bytes=64)
         nc.scalar.dma_start(x_raw[:], xT.rearrange("(p j) t -> p j t", j=PACK))
 
-        scale_table = keep.tile([P, N], U8, name="scale_table", tag="scale_table_then_x_codes", align_bytes=64)
+        scale_table = shared.tile([P, N], U8, name="scale_table", align_bytes=64, offset=4 * S - N // 2)
         nc.vector.memset(scale_table[:].bitcast(I32), 0)
         for q in range(4):
-            queue = nc.sync if q % 2 == 0 else nc.scalar
+            queue = nc.sync if q % 1 == 0 else nc.scalar
             queue.dma_start(scale_table[32 * q : 32 * q + 4, :].bitcast(I32), w_scales[0, 4 * q : 4 * q + 4, :].bitcast(I32))
 
         warm_in = keep.tile([P, 1], F32, name="warm_in", tag="warm_in_then_word_table", align_bytes=64)
@@ -58,31 +59,33 @@ def tile_picked_neuron_lin_bias_srt_p_kernel(tc, w_words, w_scales, xT, b, offs,
         w_scale = keep.tile([P, S], U8, name="w_scale", align_bytes=64)
         nc.vector.tensor_copy(w_scale[:], scale_table[:].indirect(offsets[:]))
 
-        x_bf = keep.tile([P, T, PACK], BF16, name="x_bf", tag="x_bf_then_w_codes", align_bytes=64)
+        x_bf = keep.tile([P, T, PACK], BF16, name="x_bf", align_bytes=64)
         nc.scalar.copy(x_bf[:].rearrange("p (c i) j -> p c j i", i=4), x_raw[:].rearrange("p j (c i) -> p c j i", i=4))
 
-        x_codes = keep.tile([P, T], U32, name="x_codes", tag="scale_table_then_x_codes", align_bytes=64)
+        x_codes = shared.tile([P, T], U32, name="x_codes", align_bytes=64, offset=4 * S)
         x_scale = keep.tile([P, T], U8, name="x_scale", align_bytes=64)
         nc.vector.quantize_mx(out=x_codes[:].bitcast(FP8X4), scales=x_scale[:], in_=x_bf[:].rearrange("p t j -> p (t j)"))
 
-        w_codes = keep.tile([P, S], U32, name="w_codes", tag="x_bf_then_w_codes", align_bytes=64)
+        w_codes = shared.tile([P, S], U32, name="w_codes", align_bytes=64, offset=0)
         for m in range(CHUNKS):
             reach = W_FIRST if M * (m + 1) + (N - S) <= W_FIRST else N
             cols = slice(M * m, M * (m + 1))
             nc.vector.tensor_copy(w_codes[:, cols], word_table[:, 0:reach].bitcast(U32).indirect(offsets[:, COLS * m : COLS * (m + 1)]))
-            acc = psum.tile([M, T], F32, name="acc%d" % m)
-            nc.tensor.matmul_mx(
-                out=acc[:],
-                lhsT=w_codes[:, cols].bitcast(FP8X4),
-                lhsT_scale=w_scale[:, cols],
-                rhs=x_codes[:].bitcast(FP8X4),
-                rhs_scale=x_scale[:],
-                start=True,
-                stop=True,
-            )
             result = keep.tile([M, T], F32, name="result%d" % m)
-            if m < CHUNKS - 1:
-                nc.scalar.activation(result[:], acc[:], IDENT, bias=bias[:, m : m + 1])
-            else:
-                nc.vector.tensor_scalar(result[:], acc[:], bias[:, m : m + 1], None, ADD)
+            pieces = [slice(0, T)] if m < CHUNKS - 1 else [slice(0, T // 2), slice(T // 2, T)]
+            for h, tokens in enumerate(pieces):
+                acc = psum.tile([M, tokens.stop - tokens.start], F32, name="acc%d_%d" % (m, h))
+                nc.tensor.matmul_mx(
+                    out=acc[:],
+                    lhsT=w_codes[:, cols].bitcast(FP8X4),
+                    lhsT_scale=w_scale[:, cols],
+                    rhs=x_codes[:, tokens].bitcast(FP8X4),
+                    rhs_scale=x_scale[:, tokens],
+                    start=True,
+                    stop=True,
+                )
+                if m == CHUNKS - 1 and h == 0:
+                    nc.vector.tensor_scalar(result[:, tokens], acc[:], bias[:, m : m + 1], None, ADD)
+                else:
+                    nc.scalar.activation(result[:, tokens], acc[:], IDENT, bias=bias[:, m : m + 1])
             nc.sync.dma_start(out[cols, :], result[:])

@@ -1,6 +1,7 @@
 from contextlib import ExitStack
 
 import concourse.mybir as mybir
+from concourse.masks import make_identity
 
 K, T, S, N = 512, 256, 512, 1024
 FLOPS = 2 * K * S * T
@@ -12,80 +13,89 @@ U32 = mybir.dt.uint32
 U16 = mybir.dt.uint16
 U8 = mybir.dt.uint8
 FP8X4 = mybir.dt.float8_e4m3fn_x4
-IDENT = mybir.ActivationFunctionType.Identity
+IDENTITY = mybir.ActivationFunctionType.Identity
+COPY = mybir.ActivationFunctionType.Copy
 ADD = mybir.AluOpType.add
 
 P = 128
 PACK = 4
-M = 128
-CHUNKS = S // M
-COLS = M // 16
-W_FIRST = 640
+CHUNK = 128
+CHUNKS = S // CHUNK
+CHUNK_COLS = CHUNK // 16
+QUADRANTS, QUADRANT_ROWS, SCALE_ROWS = 4, 32, 4
+HALF = T // 2
+W_FIRST = CHUNK + (N - S)
+T_VECTOR = 176
 
 
 def tile_picked_neuron_lin_bias_srt_p_kernel(tc, w_words, w_scales, xT, b, offs, out):
     nc = tc.nc
     with ExitStack() as ctx:
         keep = ctx.enter_context(tc.tile_pool(name="keep", bufs=1))
-        shared = ctx.enter_context(tc.tile_pool(name="shared", bufs=1))
         psum = ctx.enter_context(tc.psum_pool(name="psum", bufs=1))
 
+        word_table = keep.tile([P, N], I32, name="word_table", align_bytes=64)
+        w_rows = w_words[0].rearrange("p n r -> p (n r)")
+        nc.sync.dma_start(word_table[:, 0:W_FIRST], w_rows[:, 0 : PACK * W_FIRST].bitcast(I32))
         offsets = keep.tile([P, S // 16], U16, name="offsets")
         nc.sync.dma_start(offsets[:], offs)
+        nc.sync.dma_start(word_table[:, W_FIRST:N], w_rows[:, PACK * W_FIRST : PACK * N].bitcast(I32))
 
-        x_raw = keep.tile([P, PACK, T], F32, name="x_raw", align_bytes=64)
-        nc.scalar.dma_start(x_raw[:], xT.rearrange("(p j) t -> p j t", j=PACK))
+        x_raw = keep.tile([P, PACK, T], F32, name="x_raw", tag="x_raw_then_bias", align_bytes=64)
+        nc.sync.dma_start(x_raw[:], xT.rearrange("(p j) t -> p j t", j=PACK))
 
-        scale_table = shared.tile([P, N], U8, name="scale_table", align_bytes=64, offset=4 * S - N // 2)
+        bias_rows = keep.tile([P, P], F32, name="bias_rows")
+        nc.vector.memset(bias_rows[:], 0.0)
+        nc.sync.dma_start(bias_rows[0:CHUNKS, :], b.rearrange("(c p) o -> c (p o)", p=P))
+        identity = keep.tile([P, P], F32, name="identity", tag="identity_then_w_scale", align_bytes=64)
+        make_identity(nc, identity[:])
+
+        scale_table = keep.tile([P, N], U8, name="scale_table", align_bytes=64)
         nc.vector.memset(scale_table[:].bitcast(I32), 0)
-        for q in range(4):
-            queue = nc.sync if q % 1 == 0 else nc.scalar
-            queue.dma_start(scale_table[32 * q : 32 * q + 4, :].bitcast(I32), w_scales[0, 4 * q : 4 * q + 4, :].bitcast(I32))
+        for q in range(QUADRANTS):
+            nc.sync.dma_start(
+                scale_table[QUADRANT_ROWS * q : QUADRANT_ROWS * q + SCALE_ROWS, :].bitcast(I32),
+                w_scales[0, SCALE_ROWS * q : SCALE_ROWS * (q + 1), :].bitcast(I32),
+            )
 
-        warm_in = keep.tile([P, 1], F32, name="warm_in", tag="warm_in_then_word_table", align_bytes=64)
-        warm_out = keep.tile([P, 1], F32, name="warm_out", tag="warm_out_then_bias")
-        nc.vector.memset(warm_in[:], 0.0)
-        nc.scalar.activation(warm_out[:], warm_in[:], IDENT)
-
-        word_table = keep.tile([P, N], I32, name="word_table", tag="warm_in_then_word_table", align_bytes=64)
-        w_rows = w_words[0].rearrange("p n r -> p (n r)")
-        for c0, c1 in ((0, W_FIRST), (W_FIRST, N)):
-            nc.sync.dma_start(word_table[:, c0:c1], w_rows[:, 4 * c0 : 4 * c1].bitcast(I32))
-
-        bias = keep.tile([P, CHUNKS], F32, name="bias", tag="warm_out_then_bias")
-        with nc.allow_non_contiguous_dma(reason="one bias value a partition and chunk"):
-            nc.sync.dma_start(bias[:], b.rearrange("(c p) o -> p (c o)", p=P))
-
-        w_scale = keep.tile([P, S], U8, name="w_scale", align_bytes=64)
-        nc.vector.tensor_copy(w_scale[:], scale_table[:].indirect(offsets[:]))
+        w_codes = keep.tile([P, S], U32, name="w_codes", align_bytes=64)
+        nc.vector.tensor_copy(w_codes[:, 0:CHUNK], word_table[:, 0:W_FIRST].bitcast(U32).indirect(offsets[:, 0:CHUNK_COLS]))
+        nc.vector.tensor_copy(w_codes[:, CHUNK:S], word_table[:].bitcast(U32).indirect(offsets[:, CHUNK_COLS : S // 16]))
 
         x_bf = keep.tile([P, T, PACK], BF16, name="x_bf", align_bytes=64)
-        nc.scalar.copy(x_bf[:].rearrange("p (c i) j -> p c j i", i=4), x_raw[:].rearrange("p j (c i) -> p c j i", i=4))
+        grouped = lambda t0, t1: x_bf[:, t0:t1, :].rearrange("p (c i) j -> p c j i", i=4)
+        raw = lambda t0, t1: x_raw[:, :, t0:t1].rearrange("p j (c i) -> p c j i", i=4)
+        nc.vector.tensor_copy(grouped(0, T_VECTOR), raw(0, T_VECTOR))
+        nc.scalar.activation(grouped(T_VECTOR, T), raw(T_VECTOR, T), COPY)
 
-        x_codes = shared.tile([P, T], U32, name="x_codes", align_bytes=64, offset=4 * S)
+        x_codes = keep.tile([P, T], U32, name="x_codes", align_bytes=64)
         x_scale = keep.tile([P, T], U8, name="x_scale", align_bytes=64)
         nc.vector.quantize_mx(out=x_codes[:].bitcast(FP8X4), scales=x_scale[:], in_=x_bf[:].rearrange("p t j -> p (t j)"))
 
-        w_codes = shared.tile([P, S], U32, name="w_codes", align_bytes=64, offset=0)
+        bias_turned = psum.tile([P, P], F32, name="bias_turned")
+        nc.tensor.transpose(bias_turned[:], bias_rows[:], identity[:])
+        bias = keep.tile([P, CHUNKS], F32, name="bias", tag="x_raw_then_bias", align_bytes=64)
+        nc.scalar.activation(bias[:], bias_turned[:, 0:CHUNKS], COPY)
+
+        w_scale = keep.tile([P, S], U8, name="w_scale", tag="identity_then_w_scale", align_bytes=64)
         for m in range(CHUNKS):
-            reach = W_FIRST if M * (m + 1) + (N - S) <= W_FIRST else N
-            cols = slice(M * m, M * (m + 1))
-            nc.vector.tensor_copy(w_codes[:, cols], word_table[:, 0:reach].bitcast(U32).indirect(offsets[:, COLS * m : COLS * (m + 1)]))
-            result = keep.tile([M, T], F32, name="result%d" % m)
-            pieces = [slice(0, T)] if m < CHUNKS - 1 else [slice(0, T // 2), slice(T // 2, T)]
-            for h, tokens in enumerate(pieces):
-                acc = psum.tile([M, tokens.stop - tokens.start], F32, name="acc%d_%d" % (m, h))
+            entries = slice(CHUNK * m, CHUNK * (m + 1))
+            nc.vector.tensor_copy(w_scale[:, entries], scale_table[:].indirect(offsets[:, CHUNK_COLS * m : CHUNK_COLS * (m + 1)]))
+            result = keep.tile([CHUNK, T], F32, name="result%d" % m)
+            last = m == CHUNKS - 1
+            for h, tokens in enumerate([slice(0, HALF), slice(HALF, T)] if last else [slice(0, T)]):
+                acc = psum.tile([CHUNK, tokens.stop - tokens.start], F32, name="acc%d_%d" % (m, h))
                 nc.tensor.matmul_mx(
                     out=acc[:],
-                    lhsT=w_codes[:, cols].bitcast(FP8X4),
-                    lhsT_scale=w_scale[:, cols],
+                    lhsT=w_codes[:, entries].bitcast(FP8X4),
+                    lhsT_scale=w_scale[:, entries],
                     rhs=x_codes[:, tokens].bitcast(FP8X4),
                     rhs_scale=x_scale[:, tokens],
                     start=True,
                     stop=True,
                 )
-                if m == CHUNKS - 1 and h == 0:
+                if last and h == 0:
                     nc.vector.tensor_scalar(result[:, tokens], acc[:], bias[:, m : m + 1], None, ADD)
                 else:
-                    nc.scalar.activation(result[:, tokens], acc[:], IDENT, bias=bias[:, m : m + 1])
-            nc.sync.dma_start(out[cols, :], result[:])
+                    nc.scalar.activation(result[:, tokens], acc[:], IDENTITY, bias=bias[:, m : m + 1])
+            nc.sync.dma_start(out[entries, :], result[:])

@@ -25,7 +25,7 @@ CHUNK_COLS = CHUNK // 16
 QUADRANTS, QUADRANT_ROWS, SCALE_ROWS = 4, 32, 4
 HALF = T // 2
 W_FIRST = CHUNK + (N - S)
-T_VECTOR = 176
+T_VECTOR = 160
 
 
 def tile_picked_neuron_lin_bias_srt_p_kernel(tc, w_words, w_scales, xT, b, offs, out):
@@ -65,12 +65,16 @@ def tile_picked_neuron_lin_bias_srt_p_kernel(tc, w_words, w_scales, xT, b, offs,
         x_bf = keep.tile([P, T, PACK], BF16, name="x_bf", align_bytes=64)
         grouped = lambda t0, t1: x_bf[:, t0:t1, :].rearrange("p (c i) j -> p c j i", i=4)
         raw = lambda t0, t1: x_raw[:, :, t0:t1].rearrange("p j (c i) -> p c j i", i=4)
-        nc.vector.tensor_copy(grouped(0, T_VECTOR), raw(0, T_VECTOR))
+        nc.vector.tensor_copy(grouped(0, HALF), raw(0, HALF))
+        nc.vector.tensor_copy(grouped(HALF, T_VECTOR), raw(HALF, T_VECTOR))
         nc.scalar.activation(grouped(T_VECTOR, T), raw(T_VECTOR, T), COPY)
 
         x_codes = keep.tile([P, T], U32, name="x_codes", align_bytes=64)
         x_scale = keep.tile([P, T], U8, name="x_scale", align_bytes=64)
-        nc.vector.quantize_mx(out=x_codes[:].bitcast(FP8X4), scales=x_scale[:], in_=x_bf[:].rearrange("p t j -> p (t j)"))
+        for tokens in (slice(0, HALF), slice(HALF, T)):
+            nc.vector.quantize_mx(
+                out=x_codes[:, tokens].bitcast(FP8X4), scales=x_scale[:, tokens], in_=x_bf[:, tokens, :].rearrange("p t j -> p (t j)")
+            )
 
         bias_turned = psum.tile([P, P], F32, name="bias_turned")
         nc.tensor.transpose(bias_turned[:], bias_rows[:], identity[:])

@@ -1,7 +1,6 @@
 from contextlib import ExitStack
 
 import concourse.mybir as mybir
-from concourse.masks import make_identity
 
 K, T, S, N = 512, 256, 512, 1024
 FLOPS = 2 * K * S * T
@@ -16,6 +15,7 @@ FP8X4 = mybir.dt.float8_e4m3fn_x4
 IDENTITY = mybir.ActivationFunctionType.Identity
 COPY = mybir.ActivationFunctionType.Copy
 ADD = mybir.AluOpType.add
+NOT_EQUAL = mybir.AluOpType.not_equal
 
 P = 128
 PACK = 4
@@ -24,8 +24,6 @@ CHUNKS = S // CHUNK
 CHUNK_COLS = CHUNK // 16
 QUADRANTS, QUADRANT_ROWS, SCALE_ROWS = 4, 32, 4
 HALF = T // 2
-W_FIRST = CHUNK + (N - S)
-T_VECTOR = 160
 
 
 def tile_picked_neuron_lin_bias_srt_p_kernel(tc, w_words, w_scales, xT, b, offs, out):
@@ -34,21 +32,10 @@ def tile_picked_neuron_lin_bias_srt_p_kernel(tc, w_words, w_scales, xT, b, offs,
         keep = ctx.enter_context(tc.tile_pool(name="keep", bufs=1))
         psum = ctx.enter_context(tc.psum_pool(name="psum", bufs=1))
 
-        word_table = keep.tile([P, N], I32, name="word_table", align_bytes=64)
-        w_rows = w_words[0].rearrange("p n r -> p (n r)")
-        nc.sync.dma_start(word_table[:, 0:W_FIRST], w_rows[:, 0 : PACK * W_FIRST].bitcast(I32))
-        offsets = keep.tile([P, S // 16], U16, name="offsets")
-        nc.sync.dma_start(offsets[:], offs)
-        nc.sync.dma_start(word_table[:, W_FIRST:N], w_rows[:, PACK * W_FIRST : PACK * N].bitcast(I32))
-
         x_raw = keep.tile([P, PACK, T], F32, name="x_raw", tag="x_raw_then_bias", align_bytes=64)
         nc.sync.dma_start(x_raw[:], xT.rearrange("(p j) t -> p j t", j=PACK))
-
-        bias_rows = keep.tile([P, P], F32, name="bias_rows")
-        nc.vector.memset(bias_rows[:], 0.0)
-        nc.sync.dma_start(bias_rows[0:CHUNKS, :], b.rearrange("(c p) o -> c (p o)", p=P))
-        identity = keep.tile([P, P], F32, name="identity", tag="identity_then_w_scale", align_bytes=64)
-        make_identity(nc, identity[:])
+        offsets = keep.tile([P, S // 16], U16, name="offsets")
+        nc.sync.dma_start(offsets[:], offs)
 
         scale_table = keep.tile([P, N], U8, name="scale_table", align_bytes=64)
         nc.vector.memset(scale_table[:].bitcast(I32), 0)
@@ -58,33 +45,48 @@ def tile_picked_neuron_lin_bias_srt_p_kernel(tc, w_words, w_scales, xT, b, offs,
                 w_scales[0, SCALE_ROWS * q : SCALE_ROWS * (q + 1), :].bitcast(I32),
             )
 
-        w_codes = keep.tile([P, S], U32, name="w_codes", align_bytes=64)
-        nc.vector.tensor_copy(w_codes[:, 0:CHUNK], word_table[:, 0:W_FIRST].bitcast(U32).indirect(offsets[:, 0:CHUNK_COLS]))
-        nc.vector.tensor_copy(w_codes[:, CHUNK:S], word_table[:].bitcast(U32).indirect(offsets[:, CHUNK_COLS : S // 16]))
+        bias_rows = keep.tile([P, P], F32, name="bias_rows")
+        nc.vector.memset(bias_rows[:], 0.0)
+        nc.sync.dma_start(bias_rows[0:CHUNKS, :], b.rearrange("(c p) o -> c (p o)", p=P))
+
+        zeros = keep.tile([P, P], F32, name="zeros", tag="zeros_then_words", align_bytes=64)
+        nc.gpsimd.memset(zeros[:], 0.0)
+        identity = keep.tile([P, P], F32, name="identity", tag="identity_then_x_codes", align_bytes=64)
+        nc.gpsimd.affine_select(
+            out=identity[:], in_=zeros[:], compare_op=NOT_EQUAL, fill=1.0, base=0, pattern=[[-1, P]], channel_multiplier=1
+        )
+
+        word_table = keep.tile([P, N], I32, name="word_table", tag="zeros_then_words", align_bytes=64)
+        nc.sync.dma_start(word_table[:], w_words[0].rearrange("p n r -> p (n r)").bitcast(I32))
 
         x_bf = keep.tile([P, T, PACK], BF16, name="x_bf", align_bytes=64)
         grouped = lambda t0, t1: x_bf[:, t0:t1, :].rearrange("p (c i) j -> p c j i", i=4)
         raw = lambda t0, t1: x_raw[:, :, t0:t1].rearrange("p j (c i) -> p c j i", i=4)
         nc.vector.tensor_copy(grouped(0, HALF), raw(0, HALF))
-        nc.vector.tensor_copy(grouped(HALF, T_VECTOR), raw(HALF, T_VECTOR))
-        nc.scalar.activation(grouped(T_VECTOR, T), raw(T_VECTOR, T), COPY)
-
-        x_codes = keep.tile([P, T], U32, name="x_codes", align_bytes=64)
-        x_scale = keep.tile([P, T], U8, name="x_scale", align_bytes=64)
-        for tokens in (slice(0, HALF), slice(HALF, T)):
-            nc.vector.quantize_mx(
-                out=x_codes[:, tokens].bitcast(FP8X4), scales=x_scale[:, tokens], in_=x_bf[:, tokens, :].rearrange("p t j -> p (t j)")
-            )
+        nc.scalar.activation(grouped(HALF, T), raw(HALF, T), COPY)
 
         bias_turned = psum.tile([P, P], F32, name="bias_turned")
         nc.tensor.transpose(bias_turned[:], bias_rows[:], identity[:])
         bias = keep.tile([P, CHUNKS], F32, name="bias", tag="x_raw_then_bias", align_bytes=64)
         nc.scalar.activation(bias[:], bias_turned[:, 0:CHUNKS], COPY)
 
-        w_scale = keep.tile([P, S], U8, name="w_scale", tag="identity_then_w_scale", align_bytes=64)
+        w_scale = keep.tile([P, S], U8, name="w_scale", align_bytes=64)
+        nc.vector.tensor_copy(w_scale[:], scale_table[:].indirect(offsets[:]))
+
+        x_codes = keep.tile([P, T], U32, name="x_codes", tag="identity_then_x_codes", align_bytes=64)
+        x_scale = keep.tile([P, T], U8, name="x_scale", align_bytes=64)
+        for tokens in (slice(0, HALF), slice(HALF, T)):
+            nc.vector.quantize_mx(
+                out=x_codes[:, tokens].bitcast(FP8X4), scales=x_scale[:, tokens], in_=x_bf[:, tokens, :].rearrange("p t j -> p (t j)")
+            )
+
+        w_codes = keep.tile([P, S], U32, name="w_codes", align_bytes=64)
         for m in range(CHUNKS):
             entries = slice(CHUNK * m, CHUNK * (m + 1))
-            nc.vector.tensor_copy(w_scale[:, entries], scale_table[:].indirect(offsets[:, CHUNK_COLS * m : CHUNK_COLS * (m + 1)]))
+            nc.vector.tensor_copy(w_codes[:, entries], word_table[:].bitcast(U32).indirect(offsets[:, CHUNK_COLS * m : CHUNK_COLS * (m + 1)]))
+
+        for m in range(CHUNKS):
+            entries = slice(CHUNK * m, CHUNK * (m + 1))
             result = keep.tile([CHUNK, T], F32, name="result%d" % m)
             last = m == CHUNKS - 1
             for h, tokens in enumerate([slice(0, HALF), slice(HALF, T)] if last else [slice(0, T)]):
@@ -98,7 +100,7 @@ def tile_picked_neuron_lin_bias_srt_p_kernel(tc, w_words, w_scales, xT, b, offs,
                     start=True,
                     stop=True,
                 )
-                if last and h == 0:
+                if m == CHUNKS - 2 or h == 1:
                     nc.vector.tensor_scalar(result[:, tokens], acc[:], bias[:, m : m + 1], None, ADD)
                 else:
                     nc.scalar.activation(result[:, tokens], acc[:], IDENTITY, bias=bias[:, m : m + 1])

@@ -22,7 +22,7 @@ PACK = 4
 CHUNK = 128
 CHUNKS = S // CHUNK
 CHUNK_COLS = CHUNK // 16
-QUADRANTS, QUADRANT_ROWS, SCALE_ROWS = 4, 32, 4
+QUADRANT_ROWS, SCALE_ROWS = 32, 4
 HALF = T // 2
 
 
@@ -39,15 +39,8 @@ def tile_picked_neuron_lin_bias_srt_p_kernel(tc, w_words, w_scales, xT, b, offs,
 
         scale_table = keep.tile([P, N], U8, name="scale_table", align_bytes=64)
         nc.vector.memset(scale_table[:].bitcast(I32), 0)
-        for q in range(QUADRANTS):
-            nc.sync.dma_start(
-                scale_table[QUADRANT_ROWS * q : QUADRANT_ROWS * q + SCALE_ROWS, :].bitcast(I32),
-                w_scales[0, SCALE_ROWS * q : SCALE_ROWS * (q + 1), :].bitcast(I32),
-            )
-
-        bias_rows = keep.tile([P, P], F32, name="bias_rows")
-        nc.vector.memset(bias_rows[:], 0.0)
-        nc.sync.dma_start(bias_rows[0:CHUNKS, :], b.rearrange("(c p) o -> c (p o)", p=P))
+        for r in range(SCALE_ROWS):
+            nc.sync.dma_start(scale_table[r:P:QUADRANT_ROWS, :].bitcast(I32), w_scales[0, r::SCALE_ROWS, :].bitcast(I32))
 
         zeros = keep.tile([P, P], F32, name="zeros", tag="zeros_then_words", align_bytes=64)
         nc.gpsimd.memset(zeros[:], 0.0)
@@ -55,6 +48,10 @@ def tile_picked_neuron_lin_bias_srt_p_kernel(tc, w_words, w_scales, xT, b, offs,
         nc.gpsimd.affine_select(
             out=identity[:], in_=zeros[:], compare_op=NOT_EQUAL, fill=1.0, base=0, pattern=[[-1, P]], channel_multiplier=1
         )
+
+        bias_rows = keep.tile([P, P], F32, name="bias_rows")
+        nc.sync.dma_start(bias_rows[P - CHUNKS : P, :], b.rearrange("(c p) o -> c (p o)", p=P))
+        nc.vector.memset(bias_rows[0 : P - CHUNKS, :], 0.0)
 
         word_table = keep.tile([P, N], I32, name="word_table", tag="zeros_then_words", align_bytes=64)
         nc.sync.dma_start(word_table[:], w_words[0].rearrange("p n r -> p (n r)").bitcast(I32))
@@ -68,7 +65,7 @@ def tile_picked_neuron_lin_bias_srt_p_kernel(tc, w_words, w_scales, xT, b, offs,
         bias_turned = psum.tile([P, P], F32, name="bias_turned")
         nc.tensor.transpose(bias_turned[:], bias_rows[:], identity[:])
         bias = keep.tile([P, CHUNKS], F32, name="bias", tag="x_raw_then_bias", align_bytes=64)
-        nc.scalar.activation(bias[:], bias_turned[:, 0:CHUNKS], COPY)
+        nc.scalar.activation(bias[:], bias_turned[:, P - CHUNKS : P], COPY)
 
         w_scale = keep.tile([P, S], U8, name="w_scale", align_bytes=64)
         nc.vector.tensor_copy(w_scale[:], scale_table[:].indirect(offsets[:]))
@@ -89,7 +86,7 @@ def tile_picked_neuron_lin_bias_srt_p_kernel(tc, w_words, w_scales, xT, b, offs,
             entries = slice(CHUNK * m, CHUNK * (m + 1))
             result = keep.tile([CHUNK, T], F32, name="result%d" % m)
             last = m == CHUNKS - 1
-            for h, tokens in enumerate([slice(0, HALF), slice(HALF, T)] if last else [slice(0, T)]):
+            for h, tokens in enumerate([slice(0, HALF), slice(HALF, T)] if m == 0 or last else [slice(0, T)]):
                 acc = psum.tile([CHUNK, tokens.stop - tokens.start], F32, name="acc%d_%d" % (m, h))
                 nc.tensor.matmul_mx(
                     out=acc[:],
@@ -100,7 +97,7 @@ def tile_picked_neuron_lin_bias_srt_p_kernel(tc, w_words, w_scales, xT, b, offs,
                     start=True,
                     stop=True,
                 )
-                if m == CHUNKS - 2 or h == 1:
+                if m == CHUNKS - 2 or (last and h == 1):
                     nc.vector.tensor_scalar(result[:, tokens], acc[:], bias[:, m : m + 1], None, ADD)
                 else:
                     nc.scalar.activation(result[:, tokens], acc[:], IDENTITY, bias=bias[:, m : m + 1])

@@ -24,6 +24,7 @@ CHUNKS = S // CHUNK
 CHUNK_COLS = CHUNK // 16
 QUADRANT_ROWS, SCALE_ROWS = 32, 4
 HALF = T // 2
+T_VECTOR = 88
 
 
 def tile_picked_neuron_lin_bias_srt_p_kernel(tc, w_words, w_scales, xT, b, offs, out):
@@ -59,10 +60,11 @@ def tile_picked_neuron_lin_bias_srt_p_kernel(tc, w_words, w_scales, xT, b, offs,
         x_bf = keep.tile([P, T, PACK], BF16, name="x_bf", align_bytes=64)
         grouped = lambda t0, t1: x_bf[:, t0:t1, :].rearrange("p (c i) j -> p c j i", i=4)
         raw = lambda t0, t1: x_raw[:, :, t0:t1].rearrange("p j (c i) -> p c j i", i=4)
-        nc.vector.tensor_copy(grouped(0, HALF), raw(0, HALF))
+        nc.vector.tensor_copy(grouped(0, T_VECTOR), raw(0, T_VECTOR))
+        nc.scalar.activation(grouped(T_VECTOR, HALF), raw(T_VECTOR, HALF), COPY)
         nc.scalar.activation(grouped(HALF, T), raw(HALF, T), COPY)
 
-        bias_turned = psum.tile([P, P], F32, name="bias_turned")
+        bias_turned = psum.tile([P, P], F32, name="bias_turned", tag="bank%d" % (2 * CHUNKS - 1))
         nc.tensor.transpose(bias_turned[:], bias_rows[:], identity[:])
         bias = keep.tile([P, CHUNKS], F32, name="bias", tag="x_raw_then_bias", align_bytes=64)
         nc.scalar.activation(bias[:], bias_turned[:, P - CHUNKS : P], COPY)
@@ -85,9 +87,8 @@ def tile_picked_neuron_lin_bias_srt_p_kernel(tc, w_words, w_scales, xT, b, offs,
         for m in range(CHUNKS):
             entries = slice(CHUNK * m, CHUNK * (m + 1))
             result = keep.tile([CHUNK, T], F32, name="result%d" % m)
-            last = m == CHUNKS - 1
-            for h, tokens in enumerate([slice(0, HALF), slice(HALF, T)] if m == 0 or last else [slice(0, T)]):
-                acc = psum.tile([CHUNK, tokens.stop - tokens.start], F32, name="acc%d_%d" % (m, h))
+            for h, tokens in enumerate((slice(0, HALF), slice(HALF, T))):
+                acc = psum.tile([CHUNK, HALF], F32, name="acc%d_%d" % (m, h), tag="bank%d" % (2 * m + h))
                 nc.tensor.matmul_mx(
                     out=acc[:],
                     lhsT=w_codes[:, entries].bitcast(FP8X4),
@@ -97,7 +98,7 @@ def tile_picked_neuron_lin_bias_srt_p_kernel(tc, w_words, w_scales, xT, b, offs,
                     start=True,
                     stop=True,
                 )
-                if m == CHUNKS - 2 or (last and h == 1):
+                if h == 1:
                     nc.vector.tensor_scalar(result[:, tokens], acc[:], bias[:, m : m + 1], None, ADD)
                 else:
                     nc.scalar.activation(result[:, tokens], acc[:], IDENTITY, bias=bias[:, m : m + 1])

@@ -24,17 +24,22 @@ CHUNKS = S // CHUNK
 CHUNK_COLS = CHUNK // 16
 QUADRANT_ROWS, SCALE_ROWS = 32, 4
 HALF = T // 2
-T_VECTOR = 88
+BANK = 512
+W_FIRST = 2 * CHUNK + N - S
+T_FIRST, T_SECOND = 88, 56
 
 
 def tile_picked_neuron_lin_bias_srt_p_kernel(tc, w_words, w_scales, xT, b, offs, out):
     nc = tc.nc
     with ExitStack() as ctx:
         keep = ctx.enter_context(tc.tile_pool(name="keep", bufs=1))
+        early = ctx.enter_context(tc.tile_pool(name="early", bufs=1))
+        late = ctx.enter_context(tc.tile_pool(name="late", bufs=1))
         psum = ctx.enter_context(tc.psum_pool(name="psum", bufs=1))
 
         x_raw = keep.tile([P, PACK, T], F32, name="x_raw", tag="x_raw_then_bias", align_bytes=64)
         nc.sync.dma_start(x_raw[:], xT.rearrange("(p j) t -> p j t", j=PACK))
+
         offsets = keep.tile([P, S // 16], U16, name="offsets")
         nc.sync.dma_start(offsets[:], offs)
 
@@ -43,62 +48,82 @@ def tile_picked_neuron_lin_bias_srt_p_kernel(tc, w_words, w_scales, xT, b, offs,
         for r in range(SCALE_ROWS):
             nc.sync.dma_start(scale_table[r:P:QUADRANT_ROWS, :].bitcast(I32), w_scales[0, r::SCALE_ROWS, :].bitcast(I32))
 
-        zeros = keep.tile([P, P], F32, name="zeros", tag="zeros_then_words", align_bytes=64)
-        nc.gpsimd.memset(zeros[:], 0.0)
-        identity = keep.tile([P, P], F32, name="identity", tag="identity_then_x_codes", align_bytes=64)
-        nc.gpsimd.affine_select(
-            out=identity[:], in_=zeros[:], compare_op=NOT_EQUAL, fill=1.0, base=0, pattern=[[-1, P]], channel_multiplier=1
-        )
-
+        zeros = early.tile([P, P], F32, name="zeros", offset=0)
+        nc.vector.memset(zeros[:], 0.0)
         bias_rows = keep.tile([P, P], F32, name="bias_rows")
         nc.sync.dma_start(bias_rows[P - CHUNKS : P, :], b.rearrange("(c p) o -> c (p o)", p=P))
-        nc.vector.memset(bias_rows[0 : P - CHUNKS, :], 0.0)
+        nc.vector.tensor_copy(bias_rows[0 : P - CHUNKS, :], zeros[0 : P - CHUNKS, :])
 
-        word_table = keep.tile([P, N], I32, name="word_table", tag="zeros_then_words", align_bytes=64)
-        nc.sync.dma_start(word_table[:], w_words[0].rearrange("p n r -> p (n r)").bitcast(I32))
+        word_table = early.tile([P, N], I32, name="word_table", offset=0)
+        words = w_words[0].rearrange("p n r -> p (n r)").bitcast(I32)
+        nc.sync.dma_start(word_table[:, :W_FIRST], words[:, :W_FIRST])
+        nc.gpsimd.dma_start(word_table[:, W_FIRST:], words[:, W_FIRST:])
+
+        identity = late.tile([P, P], F32, name="identity", offset=0, align_bytes=64)
+        nc.gpsimd.memset(identity[:], 0.0)
+        nc.gpsimd.affine_select(
+            out=identity[:], in_=identity[:], compare_op=NOT_EQUAL, fill=1.0, base=0, pattern=[[-1, P]], channel_multiplier=1
+        )
 
         x_bf = keep.tile([P, T, PACK], BF16, name="x_bf", align_bytes=64)
         grouped = lambda t0, t1: x_bf[:, t0:t1, :].rearrange("p (c i) j -> p c j i", i=4)
         raw = lambda t0, t1: x_raw[:, :, t0:t1].rearrange("p j (c i) -> p c j i", i=4)
-        nc.vector.tensor_copy(grouped(0, T_VECTOR), raw(0, T_VECTOR))
-        nc.scalar.activation(grouped(T_VECTOR, HALF), raw(T_VECTOR, HALF), COPY)
-        nc.scalar.activation(grouped(HALF, T), raw(HALF, T), COPY)
+        nc.vector.tensor_copy(grouped(0, T_FIRST), raw(0, T_FIRST))
+        nc.scalar.activation(grouped(T_FIRST, HALF), raw(T_FIRST, HALF), COPY)
+        nc.vector.tensor_copy(grouped(HALF, HALF + T_SECOND), raw(HALF, HALF + T_SECOND))
+        nc.scalar.activation(grouped(HALF + T_SECOND, T), raw(HALF + T_SECOND, T), COPY)
 
-        bias_turned = psum.tile([P, P], F32, name="bias_turned", tag="bank%d" % (2 * CHUNKS - 1))
-        nc.tensor.transpose(bias_turned[:], bias_rows[:], identity[:])
+        bias_turned = psum.tile([P, 4 * BANK], F32, name="bias_turned", offset=0)
+        nc.tensor.transpose(bias_turned[:, :P], bias_rows[:], identity[:])
         bias = keep.tile([P, CHUNKS], F32, name="bias", tag="x_raw_then_bias", align_bytes=64)
         nc.scalar.activation(bias[:], bias_turned[:, P - CHUNKS : P], COPY)
 
-        w_scale = keep.tile([P, S], U8, name="w_scale", align_bytes=64)
-        nc.vector.tensor_copy(w_scale[:], scale_table[:].indirect(offsets[:]))
-
-        x_codes = keep.tile([P, T], U32, name="x_codes", tag="identity_then_x_codes", align_bytes=64)
+        w_scale = (
+            keep.tile([P, 2 * CHUNK], U8, name="w_scale0", align_bytes=64),
+            late.tile([P, 2 * CHUNK], U8, name="w_scale1", offset=0, align_bytes=64),
+        )
+        x_codes = keep.tile([P, T], U32, name="x_codes", align_bytes=64)
         x_scale = keep.tile([P, T], U8, name="x_scale", align_bytes=64)
-        for tokens in (slice(0, HALF), slice(HALF, T)):
+        w_codes = (
+            keep.tile([P, 2 * CHUNK], U32, name="w_codes0", align_bytes=64),
+            late.tile([P, 2 * CHUNK], U32, name="w_codes1", offset=2 * CHUNK, align_bytes=64),
+        )
+        picked = lambda m: w_codes[m // 2][:, CHUNK * (m % 2) : CHUNK * (m % 2 + 1)]
+
+        def quantise(tokens):
             nc.vector.quantize_mx(
                 out=x_codes[:, tokens].bitcast(FP8X4), scales=x_scale[:, tokens], in_=x_bf[:, tokens, :].rearrange("p t j -> p (t j)")
             )
 
-        w_codes = keep.tile([P, S], U32, name="w_codes", align_bytes=64)
-        for m in range(CHUNKS):
-            entries = slice(CHUNK * m, CHUNK * (m + 1))
-            nc.vector.tensor_copy(w_codes[:, entries], word_table[:].bitcast(U32).indirect(offsets[:, CHUNK_COLS * m : CHUNK_COLS * (m + 1)]))
+        def gather_words(m, columns):
+            window = word_table[:, :columns].bitcast(U32)
+            nc.vector.tensor_copy(picked(m), window.indirect(offsets[:, CHUNK_COLS * m : CHUNK_COLS * (m + 1)]))
+
+        def gather_scales(m0, m1):
+            nc.vector.tensor_copy(w_scale[m0 // 2][:], scale_table[:].indirect(offsets[:, CHUNK_COLS * m0 : CHUNK_COLS * m1]))
+
+        quantise(slice(0, HALF))
+        quantise(slice(HALF, T))
+        for m, columns in ((0, W_FIRST), (2, N)):
+            gather_scales(m, m + 2)
+            gather_words(m, columns)
+            gather_words(m + 1, columns)
 
         for m in range(CHUNKS):
             entries = slice(CHUNK * m, CHUNK * (m + 1))
             result = keep.tile([CHUNK, T], F32, name="result%d" % m)
             for h, tokens in enumerate((slice(0, HALF), slice(HALF, T))):
-                acc = psum.tile([CHUNK, HALF], F32, name="acc%d_%d" % (m, h), tag="bank%d" % (2 * m + h))
+                acc = psum.tile([CHUNK, HALF], F32, name="acc%d_%d" % (m, h), offset=4 * BANK * (2 * m + h))
                 nc.tensor.matmul_mx(
                     out=acc[:],
-                    lhsT=w_codes[:, entries].bitcast(FP8X4),
-                    lhsT_scale=w_scale[:, entries],
+                    lhsT=picked(m).bitcast(FP8X4),
+                    lhsT_scale=w_scale[m // 2][:, CHUNK * (m % 2) : CHUNK * (m % 2 + 1)],
                     rhs=x_codes[:, tokens].bitcast(FP8X4),
                     rhs_scale=x_scale[:, tokens],
                     start=True,
                     stop=True,
                 )
-                if h == 1:
+                if h == 1 and m > 1:
                     nc.vector.tensor_scalar(result[:, tokens], acc[:], bias[:, m : m + 1], None, ADD)
                 else:
                     nc.scalar.activation(result[:, tokens], acc[:], IDENTITY, bias=bias[:, m : m + 1])

@@ -26,7 +26,7 @@ QUADRANT_ROWS, SCALE_ROWS = 32, 4
 HALF = T // 2
 BANK = 512
 W_FIRST = 2 * CHUNK + N - S
-T_FIRST, T_SECOND = 88, 56
+T_FIRST = 88
 
 
 def tile_picked_neuron_lin_bias_srt_p_kernel(tc, w_words, w_scales, xT, b, offs, out):
@@ -37,11 +37,10 @@ def tile_picked_neuron_lin_bias_srt_p_kernel(tc, w_words, w_scales, xT, b, offs,
         late = ctx.enter_context(tc.tile_pool(name="late", bufs=1))
         psum = ctx.enter_context(tc.psum_pool(name="psum", bufs=1))
 
-        x_raw = keep.tile([P, PACK, T], F32, name="x_raw", tag="x_raw_then_bias", align_bytes=64)
-        nc.sync.dma_start(x_raw[:], xT.rearrange("(p j) t -> p j t", j=PACK))
-
         offsets = keep.tile([P, S // 16], U16, name="offsets")
         nc.sync.dma_start(offsets[:], offs)
+        x_raw = keep.tile([P, PACK, T], F32, name="x_raw", tag="x_raw_then_bias", align_bytes=64)
+        nc.sync.dma_start(x_raw[:], xT.rearrange("(p j) t -> p j t", j=PACK))
 
         scale_table = keep.tile([P, N], U8, name="scale_table", align_bytes=64)
         nc.vector.memset(scale_table[:].bitcast(I32), 0)
@@ -57,12 +56,13 @@ def tile_picked_neuron_lin_bias_srt_p_kernel(tc, w_words, w_scales, xT, b, offs,
         word_table = early.tile([P, N], I32, name="word_table", offset=0)
         words = w_words[0].rearrange("p n r -> p (n r)").bitcast(I32)
         nc.sync.dma_start(word_table[:, :W_FIRST], words[:, :W_FIRST])
-        nc.gpsimd.dma_start(word_table[:, W_FIRST:], words[:, W_FIRST:])
+        nc.sync.dma_start(word_table[:, W_FIRST:], words[:, W_FIRST:])
 
         identity = late.tile([P, P], F32, name="identity", offset=0, align_bytes=64)
-        nc.gpsimd.memset(identity[:], 0.0)
+        blank = keep.tile([P, P], F32, name="blank", tag="blank_then_x_codes", align_bytes=64)
+        nc.gpsimd.memset(blank[:], 0.0)
         nc.gpsimd.affine_select(
-            out=identity[:], in_=identity[:], compare_op=NOT_EQUAL, fill=1.0, base=0, pattern=[[-1, P]], channel_multiplier=1
+            out=identity[:], in_=blank[:], compare_op=NOT_EQUAL, fill=1.0, base=0, pattern=[[-1, P]], channel_multiplier=1
         )
 
         x_bf = keep.tile([P, T, PACK], BF16, name="x_bf", align_bytes=64)
@@ -70,8 +70,7 @@ def tile_picked_neuron_lin_bias_srt_p_kernel(tc, w_words, w_scales, xT, b, offs,
         raw = lambda t0, t1: x_raw[:, :, t0:t1].rearrange("p j (c i) -> p c j i", i=4)
         nc.vector.tensor_copy(grouped(0, T_FIRST), raw(0, T_FIRST))
         nc.scalar.activation(grouped(T_FIRST, HALF), raw(T_FIRST, HALF), COPY)
-        nc.vector.tensor_copy(grouped(HALF, HALF + T_SECOND), raw(HALF, HALF + T_SECOND))
-        nc.scalar.activation(grouped(HALF + T_SECOND, T), raw(HALF + T_SECOND, T), COPY)
+        nc.scalar.activation(grouped(HALF, T), raw(HALF, T), COPY)
 
         bias_turned = psum.tile([P, 4 * BANK], F32, name="bias_turned", offset=0)
         nc.tensor.transpose(bias_turned[:, :P], bias_rows[:], identity[:])
@@ -82,7 +81,7 @@ def tile_picked_neuron_lin_bias_srt_p_kernel(tc, w_words, w_scales, xT, b, offs,
             keep.tile([P, 2 * CHUNK], U8, name="w_scale0", align_bytes=64),
             late.tile([P, 2 * CHUNK], U8, name="w_scale1", offset=0, align_bytes=64),
         )
-        x_codes = keep.tile([P, T], U32, name="x_codes", align_bytes=64)
+        x_codes = keep.tile([P, T], U32, name="x_codes", tag="blank_then_x_codes", align_bytes=64)
         x_scale = keep.tile([P, T], U8, name="x_scale", align_bytes=64)
         w_codes = (
             keep.tile([P, 2 * CHUNK], U32, name="w_codes0", align_bytes=64),
@@ -102,12 +101,14 @@ def tile_picked_neuron_lin_bias_srt_p_kernel(tc, w_words, w_scales, xT, b, offs,
         def gather_scales(m0, m1):
             nc.vector.tensor_copy(w_scale[m0 // 2][:], scale_table[:].indirect(offsets[:, CHUNK_COLS * m0 : CHUNK_COLS * m1]))
 
+        gather_scales(0, 2)
         quantise(slice(0, HALF))
         quantise(slice(HALF, T))
-        for m, columns in ((0, W_FIRST), (2, N)):
-            gather_scales(m, m + 2)
-            gather_words(m, columns)
-            gather_words(m + 1, columns)
+        gather_words(0, W_FIRST)
+        gather_words(1, W_FIRST)
+        gather_scales(2, CHUNKS)
+        gather_words(2, N)
+        gather_words(3, N)
 
         for m in range(CHUNKS):
             entries = slice(CHUNK * m, CHUNK * (m + 1))

@@ -25,8 +25,8 @@ CHUNK_COLS = CHUNK // 16
 QUADRANT_ROWS, SCALE_ROWS = 32, 4
 HALF = T // 2
 BANK = 512
-W_FIRST = 2 * CHUNK + N - S
-T_FIRST = 88
+W_FIRST = CHUNK + N - S
+T_FIRST = 48
 
 
 def tile_picked_neuron_lin_bias_srt_p_kernel(tc, w_words, w_scales, xT, b, offs, out):
@@ -58,7 +58,7 @@ def tile_picked_neuron_lin_bias_srt_p_kernel(tc, w_words, w_scales, xT, b, offs,
         nc.sync.dma_start(word_table[:, :W_FIRST], words[:, :W_FIRST])
         nc.sync.dma_start(word_table[:, W_FIRST:], words[:, W_FIRST:])
 
-        identity = late.tile([P, P], F32, name="identity", offset=0, align_bytes=64)
+        identity = late.tile([P, P], F32, name="identity", offset=1536, align_bytes=64)
         blank = keep.tile([P, P], F32, name="blank", tag="blank_then_x_codes", align_bytes=64)
         nc.gpsimd.memset(blank[:], 0.0)
         nc.gpsimd.affine_select(
@@ -77,38 +77,37 @@ def tile_picked_neuron_lin_bias_srt_p_kernel(tc, w_words, w_scales, xT, b, offs,
         bias = keep.tile([P, CHUNKS], F32, name="bias", tag="x_raw_then_bias", align_bytes=64)
         nc.scalar.activation(bias[:], bias_turned[:, P - CHUNKS : P], COPY)
 
-        w_scale = (
-            keep.tile([P, 2 * CHUNK], U8, name="w_scale0", align_bytes=64),
-            late.tile([P, 2 * CHUNK], U8, name="w_scale1", offset=0, align_bytes=64),
+        LAST = CHUNKS - 1
+        w_scale_first = keep.tile([P, LAST * CHUNK], U8, name="w_scale_first", align_bytes=64)
+        w_scale_last = late.tile([P, CHUNK], U8, name="w_scale_last", offset=1600, align_bytes=64)
+        scales_of = lambda m: w_scale_first[:, CHUNK * m : CHUNK * (m + 1)] if m < LAST else w_scale_last[:]
+        w_codes_first = keep.tile([P, CHUNK], U32, name="w_codes_first", align_bytes=64)
+        w_codes_rest = late.tile([P, LAST * CHUNK], U32, name="w_codes_rest", offset=64, align_bytes=64)
+        picked = lambda m: w_codes_rest[:, CHUNK * (m - 1) : CHUNK * m] if m > 0 else w_codes_first[:]
+        x_codes = (
+            keep.tile([P, HALF], U32, name="x_codes0", tag="blank_then_x_codes", align_bytes=64),
+            late.tile([P, HALF], U32, name="x_codes1", offset=1984, align_bytes=64),
         )
-        x_codes = keep.tile([P, T], U32, name="x_codes", tag="blank_then_x_codes", align_bytes=64)
         x_scale = keep.tile([P, T], U8, name="x_scale", align_bytes=64)
-        w_codes = (
-            keep.tile([P, 2 * CHUNK], U32, name="w_codes0", align_bytes=64),
-            late.tile([P, 2 * CHUNK], U32, name="w_codes1", offset=2 * CHUNK, align_bytes=64),
-        )
-        picked = lambda m: w_codes[m // 2][:, CHUNK * (m % 2) : CHUNK * (m % 2 + 1)]
 
-        def quantise(tokens):
+        def quantise(h):
+            tokens = slice(HALF * h, HALF * (h + 1))
             nc.vector.quantize_mx(
-                out=x_codes[:, tokens].bitcast(FP8X4), scales=x_scale[:, tokens], in_=x_bf[:, tokens, :].rearrange("p t j -> p (t j)")
+                out=x_codes[h][:].bitcast(FP8X4), scales=x_scale[:, tokens], in_=x_bf[:, tokens, :].rearrange("p t j -> p (t j)")
             )
 
         def gather_words(m, columns):
             window = word_table[:, :columns].bitcast(U32)
             nc.vector.tensor_copy(picked(m), window.indirect(offsets[:, CHUNK_COLS * m : CHUNK_COLS * (m + 1)]))
 
-        def gather_scales(m0, m1):
-            nc.vector.tensor_copy(w_scale[m0 // 2][:], scale_table[:].indirect(offsets[:, CHUNK_COLS * m0 : CHUNK_COLS * m1]))
-
-        gather_scales(0, 2)
-        quantise(slice(0, HALF))
-        quantise(slice(HALF, T))
+        nc.vector.tensor_copy(w_scale_first[:], scale_table[:].indirect(offsets[:, : CHUNK_COLS * LAST]))
+        quantise(0)
         gather_words(0, W_FIRST)
-        gather_words(1, W_FIRST)
-        gather_scales(2, CHUNKS)
-        gather_words(2, N)
-        gather_words(3, N)
+        quantise(1)
+        for m in range(1, LAST):
+            gather_words(m, N)
+        nc.vector.tensor_copy(w_scale_last[:], scale_table[:].indirect(offsets[:, CHUNK_COLS * LAST :]))
+        gather_words(LAST, N)
 
         for m in range(CHUNKS):
             entries = slice(CHUNK * m, CHUNK * (m + 1))
@@ -118,8 +117,8 @@ def tile_picked_neuron_lin_bias_srt_p_kernel(tc, w_words, w_scales, xT, b, offs,
                 nc.tensor.matmul_mx(
                     out=acc[:],
                     lhsT=picked(m).bitcast(FP8X4),
-                    lhsT_scale=w_scale[m // 2][:, CHUNK * (m % 2) : CHUNK * (m % 2 + 1)],
-                    rhs=x_codes[:, tokens].bitcast(FP8X4),
+                    lhsT_scale=scales_of(m),
+                    rhs=x_codes[h][:].bitcast(FP8X4),
                     rhs_scale=x_scale[:, tokens],
                     start=True,
                     stop=True,

@@ -25,7 +25,7 @@ CHUNK_COLS = CHUNK // 16
 QUADRANT_ROWS, SCALE_ROWS = 32, 4
 HALF = T // 2
 BANK = 512
-W_FIRST = CHUNK + N - S
+reach = lambda m: CHUNK * (m + 1) + N - S
 T_FIRST = 48
 
 
@@ -39,6 +39,8 @@ def tile_picked_neuron_lin_bias_srt_p_kernel(tc, w_words, w_scales, xT, b, offs,
 
         offsets = keep.tile([P, S // 16], U16, name="offsets")
         nc.sync.dma_start(offsets[:], offs)
+        bias_rows = keep.tile([P, P], F32, name="bias_rows")
+        nc.scalar.dma_start(bias_rows[P - CHUNKS : P, :], b.rearrange("(c p) o -> c (p o)", p=P))
         x_raw = keep.tile([P, PACK, T], F32, name="x_raw", tag="x_raw_then_bias", align_bytes=64)
         nc.sync.dma_start(x_raw[:], xT.rearrange("(p j) t -> p j t", j=PACK))
 
@@ -49,14 +51,12 @@ def tile_picked_neuron_lin_bias_srt_p_kernel(tc, w_words, w_scales, xT, b, offs,
 
         zeros = early.tile([P, P], F32, name="zeros", offset=0)
         nc.vector.memset(zeros[:], 0.0)
-        bias_rows = keep.tile([P, P], F32, name="bias_rows")
-        nc.sync.dma_start(bias_rows[P - CHUNKS : P, :], b.rearrange("(c p) o -> c (p o)", p=P))
         nc.vector.tensor_copy(bias_rows[0 : P - CHUNKS, :], zeros[0 : P - CHUNKS, :])
 
         word_table = early.tile([P, N], I32, name="word_table", offset=0)
         words = w_words[0].rearrange("p n r -> p (n r)").bitcast(I32)
-        nc.sync.dma_start(word_table[:, :W_FIRST], words[:, :W_FIRST])
-        nc.sync.dma_start(word_table[:, W_FIRST:], words[:, W_FIRST:])
+        for c0, c1 in ((0, reach(0)), (reach(0), reach(2)), (reach(2), N)):
+            nc.sync.dma_start(word_table[:, c0:c1], words[:, c0:c1])
 
         identity = late.tile([P, P], F32, name="identity", offset=1536, align_bytes=64)
         blank = keep.tile([P, P], F32, name="blank", tag="blank_then_x_codes", align_bytes=64)
@@ -96,18 +96,18 @@ def tile_picked_neuron_lin_bias_srt_p_kernel(tc, w_words, w_scales, xT, b, offs,
                 out=x_codes[h][:].bitcast(FP8X4), scales=x_scale[:, tokens], in_=x_bf[:, tokens, :].rearrange("p t j -> p (t j)")
             )
 
-        def gather_words(m, columns):
-            window = word_table[:, :columns].bitcast(U32)
+        def gather_words(m):
+            window = word_table[:, : reach(m)].bitcast(U32)
             nc.vector.tensor_copy(picked(m), window.indirect(offsets[:, CHUNK_COLS * m : CHUNK_COLS * (m + 1)]))
 
         nc.vector.tensor_copy(w_scale_first[:], scale_table[:].indirect(offsets[:, : CHUNK_COLS * LAST]))
         quantise(0)
-        gather_words(0, W_FIRST)
+        gather_words(0)
         quantise(1)
         for m in range(1, LAST):
-            gather_words(m, N)
+            gather_words(m)
         nc.vector.tensor_copy(w_scale_last[:], scale_table[:].indirect(offsets[:, CHUNK_COLS * LAST :]))
-        gather_words(LAST, N)
+        gather_words(LAST)
 
         for m in range(CHUNKS):
             entries = slice(CHUNK * m, CHUNK * (m + 1))

from contextlib import ExitStack

import concourse.mybir as mybir

K, T, S, N = 512, 256, 512, 1024
FLOPS = 2 * K * S * T

F32 = mybir.dt.float32
BF16 = mybir.dt.bfloat16
I32 = mybir.dt.int32
U32 = mybir.dt.uint32
U16 = mybir.dt.uint16
U8 = mybir.dt.uint8
FP8X4 = mybir.dt.float8_e4m3fn_x4
IDENTITY = mybir.ActivationFunctionType.Identity
COPY = mybir.ActivationFunctionType.Copy
ADD = mybir.AluOpType.add
NOT_EQUAL = mybir.AluOpType.not_equal

P = 128
PACK = 4
CHUNK = 128
CHUNKS = S // CHUNK
CHUNK_COLS = CHUNK // 16
QUADRANT_ROWS, SCALE_ROWS = 32, 4
HALF = T // 2
BANK = 512
reach = lambda m: CHUNK * (m + 1) + N - S
T_FIRST = 48


def tile_picked_neuron_lin_bias_srt_p_kernel(tc, w_words, w_scales, xT, b, offs, out):
    nc = tc.nc
    with ExitStack() as ctx:
        keep = ctx.enter_context(tc.tile_pool(name="keep", bufs=1))
        early = ctx.enter_context(tc.tile_pool(name="early", bufs=1))
        late = ctx.enter_context(tc.tile_pool(name="late", bufs=1))
        psum = ctx.enter_context(tc.psum_pool(name="psum", bufs=1))

        offsets = keep.tile([P, S // 16], U16, name="offsets")
        nc.sync.dma_start(offsets[:], offs)
        bias_rows = keep.tile([P, P], F32, name="bias_rows")
        nc.scalar.dma_start(bias_rows[P - CHUNKS : P, :], b.rearrange("(c p) o -> c (p o)", p=P))
        x_raw = keep.tile([P, PACK, T], F32, name="x_raw", tag="x_raw_then_bias", align_bytes=64)
        nc.sync.dma_start(x_raw[:], xT.rearrange("(p j) t -> p j t", j=PACK))

        scale_table = keep.tile([P, N], U8, name="scale_table", align_bytes=64)
        nc.vector.memset(scale_table[:].bitcast(I32), 0)
        for r in range(SCALE_ROWS):
            nc.sync.dma_start(scale_table[r:P:QUADRANT_ROWS, :].bitcast(I32), w_scales[0, r::SCALE_ROWS, :].bitcast(I32))

        zeros = early.tile([P, P], F32, name="zeros", offset=0)
        nc.vector.memset(zeros[:], 0.0)
        nc.vector.tensor_copy(bias_rows[0 : P - CHUNKS, :], zeros[0 : P - CHUNKS, :])

        word_table = early.tile([P, N], I32, name="word_table", offset=0)
        words = w_words[0].rearrange("p n r -> p (n r)").bitcast(I32)
        for c0, c1 in ((0, reach(0)), (reach(0), reach(2)), (reach(2), N)):
            nc.sync.dma_start(word_table[:, c0:c1], words[:, c0:c1])

        identity = late.tile([P, P], F32, name="identity", offset=1536, align_bytes=64)
        blank = keep.tile([P, P], F32, name="blank", tag="blank_then_x_codes", align_bytes=64)
        nc.gpsimd.memset(blank[:], 0.0)
        nc.gpsimd.affine_select(
            out=identity[:], in_=blank[:], compare_op=NOT_EQUAL, fill=1.0, base=0, pattern=[[-1, P]], channel_multiplier=1
        )

        x_bf = keep.tile([P, T, PACK], BF16, name="x_bf", align_bytes=64)
        grouped = lambda t0, t1: x_bf[:, t0:t1, :].rearrange("p (c i) j -> p c j i", i=4)
        raw = lambda t0, t1: x_raw[:, :, t0:t1].rearrange("p j (c i) -> p c j i", i=4)
        nc.vector.tensor_copy(grouped(0, T_FIRST), raw(0, T_FIRST))
        nc.scalar.activation(grouped(T_FIRST, HALF), raw(T_FIRST, HALF), COPY)
        nc.scalar.activation(grouped(HALF, T), raw(HALF, T), COPY)

        bias_turned = psum.tile([P, 4 * BANK], F32, name="bias_turned", offset=0)
        nc.tensor.transpose(bias_turned[:, :P], bias_rows[:], identity[:])
        bias = keep.tile([P, CHUNKS], F32, name="bias", tag="x_raw_then_bias", align_bytes=64)
        nc.scalar.activation(bias[:], bias_turned[:, P - CHUNKS : P], COPY)

        LAST = CHUNKS - 1
        w_scale_first = keep.tile([P, LAST * CHUNK], U8, name="w_scale_first", align_bytes=64)
        w_scale_last = late.tile([P, CHUNK], U8, name="w_scale_last", offset=1600, align_bytes=64)
        scales_of = lambda m: w_scale_first[:, CHUNK * m : CHUNK * (m + 1)] if m < LAST else w_scale_last[:]
        w_codes_first = keep.tile([P, CHUNK], U32, name="w_codes_first", align_bytes=64)
        w_codes_rest = late.tile([P, LAST * CHUNK], U32, name="w_codes_rest", offset=64, align_bytes=64)
        picked = lambda m: w_codes_rest[:, CHUNK * (m - 1) : CHUNK * m] if m > 0 else w_codes_first[:]
        x_codes = (
            keep.tile([P, HALF], U32, name="x_codes0", tag="blank_then_x_codes", align_bytes=64),
            late.tile([P, HALF], U32, name="x_codes1", offset=1984, align_bytes=64),
        )
        x_scale = keep.tile([P, T], U8, name="x_scale", align_bytes=64)

        def quantise(h):
            tokens = slice(HALF * h, HALF * (h + 1))
            nc.vector.quantize_mx(
                out=x_codes[h][:].bitcast(FP8X4), scales=x_scale[:, tokens], in_=x_bf[:, tokens, :].rearrange("p t j -> p (t j)")
            )

        def gather_words(m):
            window = word_table[:, : reach(m)].bitcast(U32)
            nc.vector.tensor_copy(picked(m), window.indirect(offsets[:, CHUNK_COLS * m : CHUNK_COLS * (m + 1)]))

        nc.vector.tensor_copy(w_scale_first[:], scale_table[:].indirect(offsets[:, : CHUNK_COLS * LAST]))
        quantise(0)
        gather_words(0)
        quantise(1)
        for m in range(1, LAST):
            gather_words(m)
        nc.vector.tensor_copy(w_scale_last[:], scale_table[:].indirect(offsets[:, CHUNK_COLS * LAST :]))
        gather_words(LAST)

        for m in range(CHUNKS):
            entries = slice(CHUNK * m, CHUNK * (m + 1))
            result = keep.tile([CHUNK, T], F32, name="result%d" % m)
            for h, tokens in enumerate((slice(0, HALF), slice(HALF, T))):
                acc = psum.tile([CHUNK, HALF], F32, name="acc%d_%d" % (m, h), offset=4 * BANK * (2 * m + h))
                nc.tensor.matmul_mx(
                    out=acc[:],
                    lhsT=picked(m).bitcast(FP8X4),
                    lhsT_scale=scales_of(m),
                    rhs=x_codes[h][:].bitcast(FP8X4),
                    rhs_scale=x_scale[:, tokens],
                    start=True,
                    stop=True,
                )
                if h == 1 and m > 1:
                    nc.vector.tensor_scalar(result[:, tokens], acc[:], bias[:, m : m + 1], None, ADD)
                else:
                    nc.scalar.activation(result[:, tokens], acc[:], IDENTITY, bias=bias[:, m : m + 1])
            nc.sync.dma_start(out[entries, :], result[:])
